import numpy as np
import ml_dtypes


def mxq(x, axis, fmt="e4m3"):
    dtype, down = {"e4m3": (ml_dtypes.float8_e4m3fn, 7), "e5m2": (ml_dtypes.float8_e5m2, 14)}[fmt]
    v = np.moveaxis(np.asarray(x, np.float32).astype(ml_dtypes.bfloat16).astype(np.float64), axis, -1)
    blocks = v.reshape(v.shape[:-1] + (-1, 32))
    amax = np.abs(blocks).max(-1, keepdims=True)
    byte = np.maximum(np.where(amax > 0, np.frexp(amax)[1] - 1 + 127, 0) - down, 1)
    scale = np.exp2(byte - 127.0)
    codes = (blocks / scale).astype(np.float32).astype(dtype).astype(np.float64)
    return np.moveaxis((codes * scale).reshape(v.shape), -1, axis)


WIDE = False


def mx_kscale(k):
    if not WIDE:
        return np.ones(k)
    levels = np.array([30, -30])
    if k % 512:
        return np.exp2(np.random.permutation(np.resize(levels, k // 32))).repeat(32)
    a = np.empty((k // 512, 16))
    for p in range(k // 512):
        a[p, :8] = np.random.permutation(np.resize(levels, 8))
        for g in range(8):
            far = levels[np.abs(levels - a[p, g]) >= 10]
            a[p, g + 8] = far[np.random.randint(len(far))]
    return np.exp2(a.ravel()).repeat(32)


BF16 = ml_dtypes.bfloat16


def bf(x):
    return np.asarray(x, np.float32).astype(BF16)


def f64(x):
    return np.asarray(x).astype(np.float64)


M, N, KP, KB = 2048, 1024, 512, 1536


def setup_inputs():
    s, t = mx_kscale(KP), mx_kscale(KB)
    tail = np.exp(0.7 * np.random.standard_normal((N, KB)) - 0.49)
    return {
        "pair_corr": bf(np.random.uniform(-1.0, 1.0, (KP, M)) * s[:, None]),
        "body_corr": bf(np.random.uniform(-1.0, 1.0, (KB, M)) * t[:, None]),
        "pair_eci": bf(np.random.standard_normal((N, KP)) / np.sqrt(KP) / s),
        "body_eci": bf(np.random.standard_normal((N, KB)) * tail / np.sqrt(KB) / t),
        "field": bf(0.3 * np.random.standard_normal(M)),
        "prop": bf(1.0 + 0.3 * np.random.standard_normal(M)),
        "beta": bf(0.5 + 0.1 * np.random.standard_normal(N)),
    }


def reference(pair_corr, body_corr, pair_eci, body_eci, field, prop, beta):
    pc = mxq(f64(pair_corr), 0, "e4m3")
    pj = mxq(f64(pair_eci), 1, "e4m3")
    bc = mxq(f64(body_corr), 0, "e4m3")
    bj = mxq(f64(body_eci), 1, "e5m2")
    energy = (pc.T @ pj.T) + (bc.T @ bj.T)
    energy = energy + f64(field)[:, None]
    weight = np.exp(-f64(beta) * energy)
    return energy, f64(prop)[:, None] * weight

@@ -1,0 +1,358 @@
+from contextlib import ExitStack
+
+import concourse.mybir as mybir
+from concourse.masks import make_identity
+
+M, N, KP, KB = 2048, 1024, 512, 1536
+FLOPS = 2 * M * N * (KP + KB)
+
+F32 = mybir.dt.float32
+BF16 = mybir.dt.bfloat16
+U32 = mybir.dt.uint32
+U8 = mybir.dt.uint8
+E4M3 = mybir.dt.float8_e4m3fn_x4
+E5M2 = mybir.dt.float8_e5m2_x4
+ACT = mybir.ActivationFunctionType
+ALU = mybir.AluOpType
+
+P = 128
+PACK = 4
+K_PASS = P * PACK
+PASSES = (KP + KB) // K_PASS
+BANK = 512
+HALVES = N // BANK
+ROWS = 2
+GROUP = P * ROWS
+QUARTER = 512
+TILES = M // P
+SLOTS = 17
+SHARE = {(3, 0): 64}
+P_ON_S = [s for s in range(0, 22) if s % 2 == 0]
+LAG_T = 1
+LAG_X = 2
+LAG_P = 3
+E_ON_V = 99
+GP = False
+AHEAD = 2
+LEAD = 1
+ECI_AT = [1, 1, 1, 3, 3, 3]
+CORR_AT = [[1, 2, 4, 6], [8, 10, 12, 14], [16, 18, 20, 22]]
+ORDER = [("corr", 0), ("pair", 0), ("body", 0), ("body", 1), ("corr", 1), ("vec", 0), ("corr", 2), ("corr", 3), ("pair", 1), ("body", 2), ("body", 3)]
+FINE = 5
+E_MOD = 4
+MUL_AT = {2: 2, 3: 2, 4: 4}
+
+
+def tile_cluster_expansion_reweighting_s2_kernel(
+    tc, pair_corr, body_corr, pair_eci, body_eci, field, prop, beta, energy, weighted
+):
+    nc = tc.nc
+
+    with ExitStack() as ctx:
+        keep = ctx.enter_context(tc.tile_pool(name="keep", bufs=1))
+        ring = ctx.enter_context(tc.tile_pool(name="ring", bufs=SLOTS))
+        stage = ctx.enter_context(tc.tile_pool(name="stage", bufs=4))
+        psum = ctx.enter_context(tc.psum_pool(name="psum", bufs=8))
+        ctx.enter_context(tc.manual_schedule())
+
+        ident = keep.tile([P, P], F32)
+        make_identity(nc, ident[:])
+        vec_rows = keep.tile([P, GROUP], BF16)
+        nc.gpsimd.memset(vec_rows[:], 0.0)
+        warm = keep.tile([P, 2], F32)
+        nc.vector.memset(warm[:], 0.0)
+        nc.scalar.activation(out=warm[:, 1:2], in_=warm[:, 0:1], func=ACT.Exp)
+
+        def corr_rows(g):
+            return pair_corr if g == 0 else body_corr[(g - 1) * K_PASS : g * K_PASS, :]
+
+        raw_corr = {}
+        raw_pair = {}
+        shared = {}
+        raw_body = {}
+
+        def load_corr(g, quarters):
+            width = QUARTER * len(quarters)
+            cols = slice(quarters[0] * QUARTER, quarters[0] * QUARTER + width)
+            if len(quarters) == 2:
+                raw = ring.tile([P, PACK, width], BF16, name="raw_corr", tag="slot")
+                dst = raw[:]
+            elif g % 2 == 0:
+                raw = ring.tile([P, 2, PACK, width], BF16, name="raw_corr", tag="slot")
+                shared[quarters[0]] = raw
+                dst = raw[:, 0]
+            else:
+                dst = shared[quarters[0]][:, 1]
+            nc.sync.dma_start(out=dst, in_=corr_rows(g).rearrange("(p t) c -> p t c", t=PACK)[:, :, cols])
+            for j, q in enumerate(quarters):
+                raw_corr[g, q] = dst[:, :, j * QUARTER : (j + 1) * QUARTER]
+
+        def load_pair(h):
+            raw = keep.tile([P, 2, ROWS * KP], BF16, name="raw_pair%d" % h)
+            rows = pair_eci[h * BANK : (h + 1) * BANK, :]
+            nc.sync.dma_start(out=raw[:], in_=rows.rearrange("(b p r) k -> p b (r k)", b=2, r=ROWS))
+            raw_pair[h] = raw
+
+        def load_body(b):
+            raw = ring.tile([P, ROWS * KB], BF16, name="raw_body", tag="slot")
+            rows = body_eci[b * GROUP : (b + 1) * GROUP, :]
+            nc.sync.dma_start(out=raw[:], in_=rows.rearrange("(p r) k -> p (r k)", r=ROWS))
+            raw_body[b] = raw
+
+        beta_rows = keep.tile([P, N // P], BF16)
+
+        groups = M // GROUP
+        for kind, j in ORDER:
+            if kind == "corr":
+                load_corr(j, [0])
+            elif kind == "pair":
+                load_pair(j)
+            elif kind == "body":
+                load_body(j)
+            else:
+                nc.sync.dma_start(out=beta_rows[:], in_=beta.rearrange("(p w) -> p w", p=P))
+                nc.sync.dma_start(out=vec_rows[0:groups, :], in_=field.rearrange("(g x) -> g x", x=GROUP))
+                nc.sync.dma_start(out=vec_rows[groups : 2 * groups, :], in_=prop.rearrange("(g x) -> g x", x=GROUP))
+        for g in range(PASSES):
+            load_corr(g, [1])
+        for g in range(PASSES):
+            load_corr(g, [2, 3])
+
+        eci_codes = {}
+        eci_scales = {}
+        for g in range(PASSES):
+            for h in range(HALVES):
+                eci_codes[g, h] = keep.tile([P, BANK], U32, name="ec%d_%d" % (g, h), align_bytes=64)
+                eci_scales[g, h] = keep.tile([P, BANK], U8, name="es%d_%d" % (g, h), align_bytes=64)
+        corr_codes = {}
+        corr_scales = {}
+        for g in range(PASSES):
+            for q in range(M // QUARTER):
+                corr_codes[g, q] = keep.tile([P, QUARTER], U32, name="cc%d_%d" % (g, q), align_bytes=64)
+                corr_scales[g, q] = keep.tile([P, QUARTER], U8, name="cs%d_%d" % (g, q), align_bytes=64)
+
+        def turn_eci(g, b):
+            if g == 0:
+                words = raw_pair[b // 2][:, b % 2, :].bitcast(F32)
+                first, row = 0, KP // 2
+            else:
+                words = raw_body[b][:].bitcast(F32)
+                first, row = (g - 1) * (K_PASS // 2), KB // 2
+            bank = psum.tile([P, BANK], F32, name="bank", tag="bank")
+            for r in range(ROWS):
+                for u in range(2):
+                    start = r * row + first
+                    j = 2 * r + u
+                    nc.tensor.transpose(
+                        bank[:, j * P : (j + 1) * P], words[:, start + u : start + K_PASS // 2 : 2], ident[:]
+                    )
+            grouped = stage.tile([P, GROUP * PACK], BF16, name="eci_grouped", tag="eci_grouped", align_bytes=64)
+            nc.scalar.copy(
+                out=grouped[:].bitcast(F32).rearrange("p (n j) -> p n j", j=4),
+                in_=bank[:].rearrange("p (j n) -> p n j", j=4),
+            )
+            return grouped
+
+        def quantize_eci(g, b, grouped):
+            cols = slice((b % 2) * GROUP, (b % 2 + 1) * GROUP)
+            nc.vector.quantize_mx(
+                out=eci_codes[g, b // 2][:, cols].bitcast(E4M3 if g == 0 else E5M2),
+                scales=eci_scales[g, b // 2][:, cols],
+                in_=grouped[:],
+            )
+
+        def interleave_corr(g, q):
+            grouped = stage.tile([P, QUARTER * PACK], BF16, name="corr_grouped", tag="corr_grouped", align_bytes=64)
+            dst = grouped[:].rearrange("p (i a b t) -> p a t b i", i=ROWS, b=2, t=PACK)
+            src = raw_corr[g, q].rearrange("p t (a b i) -> p a t b i", b=2, i=ROWS)
+            share = SHARE.get((g, q), 0)
+            if share > 0:
+                nc.scalar.copy(out=dst[:, :share], in_=src[:, :share])
+            nc.vector.tensor_copy(out=dst[:, share:], in_=src[:, share:])
+            return grouped
+
+        def quantize_corr(g, q, grouped):
+            nc.vector.quantize_mx(out=corr_codes[g, q][:].bitcast(E4M3), scales=corr_scales[g, q][:], in_=grouped[:])
+
+        banks = {}
+
+        def multiply(n, h, g):
+            if g == 0:
+                banks[n, h] = psum.tile([P, BANK], F32, name="bank", tag="bank")
+            group, i = divmod(n, ROWS)
+            q, within = divmod(group, QUARTER // GROUP)
+            first = i * (QUARTER // ROWS) + within * P
+            cols = slice(first, first + P)
+            nc.tensor.matmul_mx(
+                out=banks[n, h][:],
+                lhsT=corr_codes[g, q][:, cols].bitcast(E4M3),
+                lhsT_scale=corr_scales[g, q][:, cols],
+                rhs=eci_codes[g, h][:].bitcast(E4M3 if g == 0 else E5M2),
+                rhs_scale=eci_scales[g, h][:],
+                start=(g == 0),
+                stop=(g == PASSES - 1),
+            )
+
+        def eci_group(passes, b):
+            turned = [turn_eci(g, b) for g in passes]
+            for g, grouped in zip(passes, turned):
+                quantize_eci(g, b, grouped)
+
+        beta_all = keep.tile([P, N], BF16)
+        per_row = keep.tile([P, 2 * TILES], F32)
+
+        def spread_vectors():
+            bank = psum.tile([P, BANK], F32, name="bank", tag="bank")
+            beta_words = beta_rows[:].bitcast(F32)
+            for w in range(4):
+                nc.tensor.transpose(
+                    bank[:, w * P : (w + 1) * P], beta_words[:, w : w + 1].to_broadcast([P, P]), ident[:]
+                )
+            nc.scalar.copy(
+                out=beta_all[:].bitcast(F32).rearrange("p (n w) -> p n w", w=4),
+                in_=bank[:].rearrange("p (w n) -> p n w", w=4),
+            )
+            bank = psum.tile([P, BANK], F32, name="bank", tag="bank")
+            nc.tensor.transpose(bank[:, 0:P], vec_rows[:].bitcast(F32), ident[:])
+            nc.scalar.copy(out=per_row[:], in_=bank[:, 0:TILES].bitcast(BF16))
+
+        per_quarter = QUARTER // P
+        steps = [(n, h) for h in range(HALVES) for n in range(per_quarter)]
+        steps = steps + [(n, h) for n in range(per_quarter, TILES) for h in range(HALVES)]
+        items = []
+        for kind, j in ORDER:
+            if kind == "corr":
+                items.append(("corr", j, 0))
+            elif kind == "pair":
+                items.extend([("eci", 0, 2 * j), ("eci", 0, 2 * j + 1)])
+            elif kind == "body":
+                items.extend([("eci", g, j) for g in range(1, PASSES)])
+            else:
+                items.append(("vec", 0, 0))
+        head = items[: len(items) - len(ECI_AT)]
+        prepare = {}
+        for j, item in enumerate(items[len(head) :]):
+            prepare.setdefault(ECI_AT[j], []).append(item)
+        for q in (1, 2, 3):
+            for g in range(PASSES):
+                prepare.setdefault(CORR_AT[q - 1][g], []).append(("corr", g, q))
+
+        def lay_out(item):
+            kind, g, j = item
+            if kind == "eci":
+                return (quantize_eci, g, j, turn_eci(g, j))
+            return (quantize_corr, g, j, interleave_corr(g, j))
+
+        def quantize(laid):
+            laid[0](*laid[1:])
+
+        c0 = lay_out(("corr", 0, 0))
+        pair = [lay_out(("eci", 0, b)) for b in (0, 1)]
+        quantize(c0)
+        for laid in pair:
+            quantize(laid)
+        for laid in [lay_out(("eci", g, 0)) for g in (1, 2, 3)]:
+            quantize(laid)
+        c1 = lay_out(("corr", 1, 0))
+        body = [lay_out(("eci", g, 1)) for g in (1, 2, 3)]
+        spread_vectors()
+        quantize(body[0])
+        quantize(c1)
+        quantize(body[1])
+        quantize(body[2])
+        for g in range(2):
+            for s in range(AHEAD):
+                multiply(steps[s][0], steps[s][1], g)
+        c2 = lay_out(("corr", 2, 0))
+        c3 = lay_out(("corr", 3, 0))
+        pending = [lay_out(("eci", 0, b)) for b in (2, 3)]
+        quantize(c2)
+        quantize(c3)
+        for s in range(AHEAD):
+            for g in range(2, PASSES):
+                multiply(steps[s][0], steps[s][1], g)
+
+        e_tiles = {}
+        w_tiles = {}
+        done = {}
+
+        def rows_of(out, group):
+            return out[group * GROUP : (group + 1) * GROUP, :].rearrange("(p i) d -> p i d", i=ROWS)
+
+        def piece(tiles, s):
+            n, h = steps[s]
+            return tiles[n // ROWS][:, n % ROWS, h * BANK : (h + 1) * BANK]
+
+        def store_if_whole(out, tiles, s, key):
+            group = steps[s][0] // ROWS
+            done[key, group] = done.get((key, group), 0) + 1
+            if group >= FINE:
+                n, h = steps[s]
+                if h == HALVES - 1:
+                    nc.sync.dma_start(out=rows_of(out, group)[:, n % ROWS, :], in_=tiles[group][:, n % ROWS, :])
+            elif done[key, group] == ROWS * HALVES:
+                nc.sync.dma_start(out=rows_of(out, group), in_=tiles[group][:])
+
+        def multiply_step(s):
+            for g in range(PASSES):
+                multiply(steps[s][0], steps[s][1], g)
+
+        def add_field(s):
+            n, h = steps[s]
+            if n // ROWS not in e_tiles:
+                e_tiles[n // ROWS] = ring.tile([P, ROWS, N], F32, name="e_tile", tag="slot")
+                w_tiles[n // ROWS] = ring.tile([P, ROWS, N], F32, name="w_tile", tag="slot")
+            if s >= E_ON_V and s % E_MOD == 1:
+                nc.vector.tensor_scalar(
+                    out=piece(e_tiles, s), in0=banks[n, h][:], scalar1=per_row[:, n : n + 1], scalar2=None, op0=ALU.add
+                )
+            else:
+                nc.scalar.activation(
+                    out=piece(e_tiles, s), in_=banks[n, h][:], func=ACT.Identity, bias=per_row[:, n : n + 1]
+                )
+            store_if_whole(energy, e_tiles, s, 0)
+
+        def times_beta(s):
+            n, h = steps[s]
+            if GP:
+                nc.vector.scalar_tensor_tensor(
+                    out=piece(w_tiles, s), in0=banks[n, h][:], scalar=per_row[:, n : n + 1],
+                    in1=beta_all[:, h * BANK : (h + 1) * BANK], op0=ALU.add, op1=ALU.mult,
+                )
+            else:
+                nc.vector.tensor_tensor(
+                    out=piece(w_tiles, s), in0=piece(e_tiles, s), in1=beta_all[:, h * BANK : (h + 1) * BANK], op=ALU.mult
+                )
+
+        def exponentiate(s):
+            w = piece(w_tiles, s)
+            nc.scalar.activation(out=w, in_=w, func=ACT.Exp, scale=-1.0)
+
+        def times_prop(s):
+            n = steps[s][0]
+            w = piece(w_tiles, s)
+            if GP:
+                nc.gpsimd.tensor_scalar(
+                    out=w, in0=w, scalar1=per_row[:, TILES + n : TILES + n + 1], scalar2=0.0, op0=ALU.mult, op1=ALU.add
+                )
+            elif s in P_ON_S:
+                nc.scalar.activation(out=w, in_=w, func=ACT.Identity, scale=per_row[:, TILES + n : TILES + n + 1])
+            else:
+                nc.vector.tensor_scalar(
+                    out=w, in0=w, scalar1=per_row[:, TILES + n : TILES + n + 1], scalar2=None, op0=ALU.mult
+                )
+            store_if_whole(weighted, w_tiles, s, 1)
+
+        issued = AHEAD
+        for s in range(len(steps) + LAG_P):
+            if 0 <= s - LAG_T < len(steps):
+                times_beta(s - LAG_T)
+            for laid in pending:
+                quantize(laid)
+            while issued < len(steps) and MUL_AT.get(issued, issued - LEAD) <= s:
+                multiply_step(issued)
+                issued = issued + 1
+            for stage_fn, lag in [(exponentiate, LAG_X), (add_field, 0), (times_prop, LAG_P)]:
+                if 0 <= s - lag < len(steps):
+                    stage_fn(s - lag)
+            pending = [lay_out(item) for item in prepare.get(s, [])]

@@ -21,26 +21,23 @@ K_PASS = P * PACK
 PASSES = (KP + KB) // K_PASS
 BANK = 512
 HALVES = N // BANK
-ROWS = 2
-GROUP = P * ROWS
-QUARTER = 512
+BLOCK = 256
 TILES = M // P
-SLOTS = 17
-SHARE = {(3, 0): 64}
-P_ON_S = [s for s in range(0, 22) if s % 2 == 0]
+LOADS = [(0, 512), (512, 512), (1024, 1024)]
+SLOTS = 15
 LAG_T = 1
 LAG_X = 2
 LAG_P = 3
-E_ON_V = 99
-GP = False
+WLAG = (1, 1, 2)
 AHEAD = 2
 LEAD = 1
-ECI_AT = [1, 1, 1, 3, 3, 3]
-CORR_AT = [[1, 2, 4, 6], [8, 10, 12, 14], [16, 18, 20, 22]]
-ORDER = [("corr", 0), ("pair", 0), ("body", 0), ("body", 1), ("corr", 1), ("vec", 0), ("corr", 2), ("corr", 3), ("pair", 1), ("body", 2), ("body", 3)]
-FINE = 5
-E_MOD = 4
+SUM_BANKS = 4
+CORR_AT = [2, 4, 6, 8, 9, 10, 11, 12, 13, 14, 15, 16]
+P_ON_S = [4, 5, 6, 7, 8, 10, 12, 14]
+ECI_AT = {1: 2, 3: 3}
 MUL_AT = {2: 2, 3: 2, 4: 4}
+HEAD_S = (True, True)
+E_ON_V = []
 
 
 def tile_cluster_expansion_reweighting_s2_kernel(
@@ -52,84 +49,78 @@ def tile_cluster_expansion_reweighting_s2_kernel(
         keep = ctx.enter_context(tc.tile_pool(name="keep", bufs=1))
         ring = ctx.enter_context(tc.tile_pool(name="ring", bufs=SLOTS))
         stage = ctx.enter_context(tc.tile_pool(name="stage", bufs=4))
-        psum = ctx.enter_context(tc.psum_pool(name="psum", bufs=8))
+        turn_banks = ctx.enter_context(tc.psum_pool(name="turn_banks", bufs=8 - SUM_BANKS))
+        sum_banks = ctx.enter_context(tc.psum_pool(name="sum_banks", bufs=SUM_BANKS))
         ctx.enter_context(tc.manual_schedule())
 
         ident = keep.tile([P, P], F32)
         make_identity(nc, ident[:])
-        vec_rows = keep.tile([P, GROUP], BF16)
+        ident_bf16 = keep.tile([P, P], BF16)
+        make_identity(nc, ident_bf16[:])
+        vec_rows = keep.tile([P, P], BF16)
         nc.gpsimd.memset(vec_rows[:], 0.0)
         warm = keep.tile([P, 2], F32)
         nc.vector.memset(warm[:], 0.0)
         nc.scalar.activation(out=warm[:, 1:2], in_=warm[:, 0:1], func=ACT.Exp)
 
-        def corr_rows(g):
-            return pair_corr if g == 0 else body_corr[(g - 1) * K_PASS : g * K_PASS, :]
-
         raw_corr = {}
+        raw_two = {}
         raw_pair = {}
-        shared = {}
         raw_body = {}
+        beta_rows = keep.tile([P, N // P], BF16)
 
-        def load_corr(g, quarters):
-            width = QUARTER * len(quarters)
-            cols = slice(quarters[0] * QUARTER, quarters[0] * QUARTER + width)
-            if len(quarters) == 2:
-                raw = ring.tile([P, PACK, width], BF16, name="raw_corr", tag="slot")
-                dst = raw[:]
-            elif g % 2 == 0:
-                raw = ring.tile([P, 2, PACK, width], BF16, name="raw_corr", tag="slot")
-                shared[quarters[0]] = raw
-                dst = raw[:, 0]
-            else:
-                dst = shared[quarters[0]][:, 1]
-            nc.sync.dma_start(out=dst, in_=corr_rows(g).rearrange("(p t) c -> p t c", t=PACK)[:, :, cols])
-            for j, q in enumerate(quarters):
-                raw_corr[g, q] = dst[:, :, j * QUARTER : (j + 1) * QUARTER]
+        def load_corr(g, first, width):
+            rows = pair_corr if g == 0 else body_corr[(g - 1) * K_PASS : g * K_PASS, :]
+            if g % 2 == 0:
+                raw_two[first] = keep.tile([P, 2, PACK, width], BF16, name="raw_corr%d_%d" % (g, first))
+            raw = raw_two[first]
+            nc.sync.dma_start(
+                out=raw[:, g % 2], in_=rows.rearrange("(p t) c -> p t c", t=PACK)[:, :, first : first + width]
+            )
+            for c in range(0, width, BLOCK):
+                raw_corr[g // 2, (first + c) // BLOCK] = raw[:, :, :, c : c + BLOCK]
 
         def load_pair(h):
-            raw = keep.tile([P, 2, ROWS * KP], BF16, name="raw_pair%d" % h)
+            raw = ring.tile([P, 2, 2 * KP], BF16, name="raw_pair", tag="slot")
             rows = pair_eci[h * BANK : (h + 1) * BANK, :]
-            nc.sync.dma_start(out=raw[:], in_=rows.rearrange("(b p r) k -> p b (r k)", b=2, r=ROWS))
+            nc.sync.dma_start(out=raw[:], in_=rows.rearrange("(b p r) k -> p b (r k)", b=2, r=2))
             raw_pair[h] = raw
 
         def load_body(b):
-            raw = ring.tile([P, ROWS * KB], BF16, name="raw_body", tag="slot")
-            rows = body_eci[b * GROUP : (b + 1) * GROUP, :]
-            nc.sync.dma_start(out=raw[:], in_=rows.rearrange("(p r) k -> p (r k)", r=ROWS))
+            raw = keep.tile([P, 2 * KB], BF16, name="raw_body%d" % b)
+            rows = body_eci[b * BLOCK : (b + 1) * BLOCK, :]
+            nc.sync.dma_start(out=raw[:], in_=rows.rearrange("(p r) k -> p (r k)", r=2))
             raw_body[b] = raw
 
-        beta_rows = keep.tile([P, N // P], BF16)
-
-        groups = M // GROUP
-        for kind, j in ORDER:
-            if kind == "corr":
-                load_corr(j, [0])
-            elif kind == "pair":
-                load_pair(j)
-            elif kind == "body":
-                load_body(j)
-            else:
-                nc.sync.dma_start(out=beta_rows[:], in_=beta.rearrange("(p w) -> p w", p=P))
-                nc.sync.dma_start(out=vec_rows[0:groups, :], in_=field.rearrange("(g x) -> g x", x=GROUP))
-                nc.sync.dma_start(out=vec_rows[groups : 2 * groups, :], in_=prop.rearrange("(g x) -> g x", x=GROUP))
-        for g in range(PASSES):
-            load_corr(g, [1])
-        for g in range(PASSES):
-            load_corr(g, [2, 3])
+        load_corr(0, *LOADS[0])
+        load_pair(0)
+        load_body(0)
+        load_body(1)
+        load_corr(1, *LOADS[0])
+        nc.sync.dma_start(out=beta_rows[:], in_=beta.rearrange("(p w) -> p w", p=P))
+        nc.sync.dma_start(out=vec_rows[0:TILES, :], in_=field.rearrange("(n p) -> n p", p=P))
+        nc.sync.dma_start(out=vec_rows[TILES : 2 * TILES, :], in_=prop.rearrange("(n p) -> n p", p=P))
+        load_corr(2, *LOADS[0])
+        load_corr(3, *LOADS[0])
+        load_pair(1)
+        load_body(2)
+        load_body(3)
+        for first, width in LOADS[1:]:
+            for g in range(PASSES):
+                load_corr(g, first, width)
 
         eci_codes = {}
         eci_scales = {}
+        corr_codes = {}
+        corr_scales = {}
         for g in range(PASSES):
             for h in range(HALVES):
                 eci_codes[g, h] = keep.tile([P, BANK], U32, name="ec%d_%d" % (g, h), align_bytes=64)
                 eci_scales[g, h] = keep.tile([P, BANK], U8, name="es%d_%d" % (g, h), align_bytes=64)
-        corr_codes = {}
-        corr_scales = {}
-        for g in range(PASSES):
-            for q in range(M // QUARTER):
-                corr_codes[g, q] = keep.tile([P, QUARTER], U32, name="cc%d_%d" % (g, q), align_bytes=64)
-                corr_scales[g, q] = keep.tile([P, QUARTER], U8, name="cs%d_%d" % (g, q), align_bytes=64)
+        for two in range(PASSES // 2):
+            for b in range(M // BLOCK):
+                corr_codes[two, b] = keep.tile([P, 2 * BLOCK], U32, name="cc%d_%d" % (two, b), align_bytes=64)
+                corr_scales[two, b] = keep.tile([P, 2 * BLOCK], U8, name="cs%d_%d" % (two, b), align_bytes=64)
 
         def turn_eci(g, b):
             if g == 0:
@@ -138,71 +129,69 @@ def tile_cluster_expansion_reweighting_s2_kernel(
             else:
                 words = raw_body[b][:].bitcast(F32)
                 first, row = (g - 1) * (K_PASS // 2), KB // 2
-            bank = psum.tile([P, BANK], F32, name="bank", tag="bank")
-            for r in range(ROWS):
+            bank = turn_banks.tile([P, BANK], F32, name="turned")
+            for r in range(2):
                 for u in range(2):
                     start = r * row + first
                     j = 2 * r + u
                     nc.tensor.transpose(
                         bank[:, j * P : (j + 1) * P], words[:, start + u : start + K_PASS // 2 : 2], ident[:]
                     )
-            grouped = stage.tile([P, GROUP * PACK], BF16, name="eci_grouped", tag="eci_grouped", align_bytes=64)
+            grouped = stage.tile([P, BLOCK * PACK], BF16, name="eci_grouped", align_bytes=64)
             nc.scalar.copy(
                 out=grouped[:].bitcast(F32).rearrange("p (n j) -> p n j", j=4),
                 in_=bank[:].rearrange("p (j n) -> p n j", j=4),
             )
-            return grouped
+            cols = slice((b % 2) * BLOCK, (b % 2 + 1) * BLOCK)
+            return eci_codes[g, b // 2][:, cols].bitcast(E4M3 if g == 0 else E5M2), eci_scales[g, b // 2][:, cols], grouped
 
-        def quantize_eci(g, b, grouped):
-            cols = slice((b % 2) * GROUP, (b % 2 + 1) * GROUP)
-            nc.vector.quantize_mx(
-                out=eci_codes[g, b // 2][:, cols].bitcast(E4M3 if g == 0 else E5M2),
-                scales=eci_scales[g, b // 2][:, cols],
-                in_=grouped[:],
-            )
+        def interleave_corr(passes, b, on_scalar=False):
+            two, first = divmod(passes[0], 2)
+            count = len(passes)
+            grouped = stage.tile([P, count * BLOCK * PACK], BF16, name="corr_grouped", bufs=4, align_bytes=64)
+            dst = grouped[:].rearrange("p (g c i t) -> p g c t i", g=count, i=4, t=PACK)
+            src = raw_corr[two, b][:, first : first + count].rearrange("p g t (c i) -> p g c t i", i=4)
+            if on_scalar:
+                nc.scalar.copy(out=dst, in_=src)
+            else:
+                nc.vector.tensor_copy(out=dst, in_=src)
+            cols = slice(first * BLOCK, (first + count) * BLOCK)
+            return corr_codes[two, b][:, cols].bitcast(E4M3), corr_scales[two, b][:, cols], grouped
 
-        def interleave_corr(g, q):
-            grouped = stage.tile([P, QUARTER * PACK], BF16, name="corr_grouped", tag="corr_grouped", align_bytes=64)
-            dst = grouped[:].rearrange("p (i a b t) -> p a t b i", i=ROWS, b=2, t=PACK)
-            src = raw_corr[g, q].rearrange("p t (a b i) -> p a t b i", b=2, i=ROWS)
-            share = SHARE.get((g, q), 0)
-            if share > 0:
-                nc.scalar.copy(out=dst[:, :share], in_=src[:, :share])
-            nc.vector.tensor_copy(out=dst[:, share:], in_=src[:, share:])
-            return grouped
+        def quantize(laid):
+            codes, scales, grouped = laid
+            nc.vector.quantize_mx(out=codes, scales=scales, in_=grouped[:])
 
-        def quantize_corr(g, q, grouped):
-            nc.vector.quantize_mx(out=corr_codes[g, q][:].bitcast(E4M3), scales=corr_scales[g, q][:], in_=grouped[:])
+        first_tiles = LOADS[0][1] // P
+        steps = [(n, (h,)) for h in range(HALVES) for n in range(first_tiles)]
+        steps = steps + [(n, (0, 1)) for n in range(first_tiles, TILES - 1)]
+        steps = steps + [(TILES - 1, (h,)) for h in range(HALVES)]
+        sums = {}
 
-        banks = {}
-
-        def multiply(n, h, g):
-            if g == 0:
-                banks[n, h] = psum.tile([P, BANK], F32, name="bank", tag="bank")
-            group, i = divmod(n, ROWS)
-            q, within = divmod(group, QUARTER // GROUP)
-            first = i * (QUARTER // ROWS) + within * P
-            cols = slice(first, first + P)
-            nc.tensor.matmul_mx(
-                out=banks[n, h][:],
-                lhsT=corr_codes[g, q][:, cols].bitcast(E4M3),
-                lhsT_scale=corr_scales[g, q][:, cols],
-                rhs=eci_codes[g, h][:].bitcast(E4M3 if g == 0 else E5M2),
-                rhs_scale=eci_scales[g, h][:],
-                start=(g == 0),
-                stop=(g == PASSES - 1),
-            )
-
-        def eci_group(passes, b):
-            turned = [turn_eci(g, b) for g in passes]
-            for g, grouped in zip(passes, turned):
-                quantize_eci(g, b, grouped)
+        def multiply(s, passes):
+            n, halves = steps[s]
+            b, i = divmod(n, BLOCK // P)
+            for h in halves:
+                for g in passes:
+                    if g == 0:
+                        sums[n, h] = sum_banks.tile([P, BANK], F32, name="sums")
+                    first = (g % 2) * BLOCK + i * P
+                    cols = slice(first, first + P)
+                    nc.tensor.matmul_mx(
+                        out=sums[n, h][:],
+                        lhsT=corr_codes[g // 2, b][:, cols].bitcast(E4M3),
+                        lhsT_scale=corr_scales[g // 2, b][:, cols],
+                        rhs=eci_codes[g, h][:].bitcast(E4M3 if g == 0 else E5M2),
+                        rhs_scale=eci_scales[g, h][:],
+                        start=(g == 0),
+                        stop=(g == PASSES - 1),
+                    )
 
         beta_all = keep.tile([P, N], BF16)
         per_row = keep.tile([P, 2 * TILES], F32)
 
         def spread_vectors():
-            bank = psum.tile([P, BANK], F32, name="bank", tag="bank")
+            bank = turn_banks.tile([P, BANK], F32, name="turned")
             beta_words = beta_rows[:].bitcast(F32)
             for w in range(4):
                 nc.tensor.transpose(
@@ -212,117 +201,72 @@ def tile_cluster_expansion_reweighting_s2_kernel(
                 out=beta_all[:].bitcast(F32).rearrange("p (n w) -> p n w", w=4),
                 in_=bank[:].rearrange("p (w n) -> p n w", w=4),
             )
-            bank = psum.tile([P, BANK], F32, name="bank", tag="bank")
-            nc.tensor.transpose(bank[:, 0:P], vec_rows[:].bitcast(F32), ident[:])
-            nc.scalar.copy(out=per_row[:], in_=bank[:, 0:TILES].bitcast(BF16))
+            bank = turn_banks.tile([P, BANK], F32, name="turned")
+            columns = bank[:, 0 : P // 2].bitcast(BF16)
+            nc.tensor.transpose(columns, vec_rows[:], ident_bf16[:])
+            nc.scalar.copy(out=per_row[:], in_=columns[:, 0 : 2 * TILES])
 
-        per_quarter = QUARTER // P
-        steps = [(n, h) for h in range(HALVES) for n in range(per_quarter)]
-        steps = steps + [(n, h) for n in range(per_quarter, TILES) for h in range(HALVES)]
-        items = []
-        for kind, j in ORDER:
-            if kind == "corr":
-                items.append(("corr", j, 0))
-            elif kind == "pair":
-                items.extend([("eci", 0, 2 * j), ("eci", 0, 2 * j + 1)])
-            elif kind == "body":
-                items.extend([("eci", g, j) for g in range(1, PASSES)])
-            else:
-                items.append(("vec", 0, 0))
-        head = items[: len(items) - len(ECI_AT)]
-        prepare = {}
-        for j, item in enumerate(items[len(head) :]):
-            prepare.setdefault(ECI_AT[j], []).append(item)
-        for q in (1, 2, 3):
-            for g in range(PASSES):
-                prepare.setdefault(CORR_AT[q - 1][g], []).append(("corr", g, q))
-
-        def lay_out(item):
-            kind, g, j = item
-            if kind == "eci":
-                return (quantize_eci, g, j, turn_eci(g, j))
-            return (quantize_corr, g, j, interleave_corr(g, j))
-
-        def quantize(laid):
-            laid[0](*laid[1:])
-
-        c0 = lay_out(("corr", 0, 0))
-        pair = [lay_out(("eci", 0, b)) for b in (0, 1)]
-        quantize(c0)
-        for laid in pair:
+        c0 = [interleave_corr((0,), b) for b in (0, 1)]
+        pair = [turn_eci(0, b) for b in (0, 1)]
+        for laid in c0 + pair:
             quantize(laid)
-        for laid in [lay_out(("eci", g, 0)) for g in (1, 2, 3)]:
+        for laid in [turn_eci(g, 0) for g in (1, 2, 3)]:
             quantize(laid)
-        c1 = lay_out(("corr", 1, 0))
-        body = [lay_out(("eci", g, 1)) for g in (1, 2, 3)]
+        body = [turn_eci(g, 1) for g in (1, 2, 3)]
+        c1 = [interleave_corr((1,), b) for b in (0, 1)]
         spread_vectors()
-        quantize(body[0])
-        quantize(c1)
-        quantize(body[1])
-        quantize(body[2])
-        for g in range(2):
-            for s in range(AHEAD):
-                multiply(steps[s][0], steps[s][1], g)
-        c2 = lay_out(("corr", 2, 0))
-        c3 = lay_out(("corr", 3, 0))
-        pending = [lay_out(("eci", 0, b)) for b in (2, 3)]
+        for laid in [body[0], c1[0], body[1], c1[1], body[2]]:
+            quantize(laid)
+        for s in range(AHEAD):
+            multiply(s, (0, 1))
+        c2 = interleave_corr((2,), 0)
+        c2_late = interleave_corr((2,), 1, HEAD_S[0])
+        c3 = interleave_corr((3,), 0)
         quantize(c2)
+        c3_late = interleave_corr((3,), 1, HEAD_S[1])
+        pair = [turn_eci(0, b) for b in (2, 3)]
         quantize(c3)
         for s in range(AHEAD):
-            for g in range(2, PASSES):
-                multiply(steps[s][0], steps[s][1], g)
+            multiply(s, (2, 3))
+        pending = [c2_late, c3_late] + pair
+
+        later = [(passes, b) for b in range(LOADS[0][1] // BLOCK, M // BLOCK) for passes in ((0, 1), (2, 3))]
+        corr_at = dict(zip(CORR_AT, later))
 
         e_tiles = {}
         w_tiles = {}
-        done = {}
 
-        def rows_of(out, group):
-            return out[group * GROUP : (group + 1) * GROUP, :].rearrange("(p i) d -> p i d", i=ROWS)
+        def draws(s):
+            halves = steps[s][1]
+            return slice(halves[0] * BANK, (halves[-1] + 1) * BANK)
 
         def piece(tiles, s):
-            n, h = steps[s]
-            return tiles[n // ROWS][:, n % ROWS, h * BANK : (h + 1) * BANK]
+            return tiles[steps[s][0]][:, draws(s)]
 
-        def store_if_whole(out, tiles, s, key):
-            group = steps[s][0] // ROWS
-            done[key, group] = done.get((key, group), 0) + 1
-            if group >= FINE:
-                n, h = steps[s]
-                if h == HALVES - 1:
-                    nc.sync.dma_start(out=rows_of(out, group)[:, n % ROWS, :], in_=tiles[group][:, n % ROWS, :])
-            elif done[key, group] == ROWS * HALVES:
-                nc.sync.dma_start(out=rows_of(out, group), in_=tiles[group][:])
-
-        def multiply_step(s):
-            for g in range(PASSES):
-                multiply(steps[s][0], steps[s][1], g)
+        def store(out, tiles, s):
+            n, halves = steps[s]
+            if n == TILES - 1:
+                nc.sync.dma_start(out=out[n * P : (n + 1) * P, draws(s)], in_=piece(tiles, s))
+            elif halves[-1] == HALVES - 1:
+                nc.sync.dma_start(out=out[n * P : (n + 1) * P, :], in_=tiles[n][:])
 
         def add_field(s):
-            n, h = steps[s]
-            if n // ROWS not in e_tiles:
-                e_tiles[n // ROWS] = ring.tile([P, ROWS, N], F32, name="e_tile", tag="slot")
-                w_tiles[n // ROWS] = ring.tile([P, ROWS, N], F32, name="w_tile", tag="slot")
-            if s >= E_ON_V and s % E_MOD == 1:
-                nc.vector.tensor_scalar(
-                    out=piece(e_tiles, s), in0=banks[n, h][:], scalar1=per_row[:, n : n + 1], scalar2=None, op0=ALU.add
-                )
-            else:
-                nc.scalar.activation(
-                    out=piece(e_tiles, s), in_=banks[n, h][:], func=ACT.Identity, bias=per_row[:, n : n + 1]
-                )
-            store_if_whole(energy, e_tiles, s, 0)
+            n, halves = steps[s]
+            if halves[0] == 0:
+                e_tiles[n] = ring.tile([P, N], F32, name="e_tile", tag="slot")
+                w_tiles[n] = ring.tile([P, N], F32, name="w_tile", tag="slot")
+            for h in halves:
+                e = e_tiles[n][:, h * BANK : (h + 1) * BANK]
+                if (n, h) in E_ON_V:
+                    nc.vector.tensor_scalar(
+                        out=e, in0=sums[n, h][:], scalar1=per_row[:, n : n + 1], scalar2=None, op0=ALU.add
+                    )
+                else:
+                    nc.scalar.activation(out=e, in_=sums[n, h][:], func=ACT.Identity, bias=per_row[:, n : n + 1])
+            store(energy, e_tiles, s)
 
         def times_beta(s):
-            n, h = steps[s]
-            if GP:
-                nc.vector.scalar_tensor_tensor(
-                    out=piece(w_tiles, s), in0=banks[n, h][:], scalar=per_row[:, n : n + 1],
-                    in1=beta_all[:, h * BANK : (h + 1) * BANK], op0=ALU.add, op1=ALU.mult,
-                )
-            else:
-                nc.vector.tensor_tensor(
-                    out=piece(w_tiles, s), in0=piece(e_tiles, s), in1=beta_all[:, h * BANK : (h + 1) * BANK], op=ALU.mult
-                )
+            nc.vector.tensor_tensor(out=piece(w_tiles, s), in0=piece(e_tiles, s), in1=beta_all[:, draws(s)], op=ALU.mult)
 
         def exponentiate(s):
             w = piece(w_tiles, s)
@@ -331,17 +275,12 @@ def tile_cluster_expansion_reweighting_s2_kernel(
         def times_prop(s):
             n = steps[s][0]
             w = piece(w_tiles, s)
-            if GP:
-                nc.gpsimd.tensor_scalar(
-                    out=w, in0=w, scalar1=per_row[:, TILES + n : TILES + n + 1], scalar2=0.0, op0=ALU.mult, op1=ALU.add
-                )
-            elif s in P_ON_S:
-                nc.scalar.activation(out=w, in_=w, func=ACT.Identity, scale=per_row[:, TILES + n : TILES + n + 1])
+            factor = per_row[:, TILES + n : TILES + n + 1]
+            if s in P_ON_S:
+                nc.scalar.activation(out=w, in_=w, func=ACT.Identity, scale=factor)
             else:
-                nc.vector.tensor_scalar(
-                    out=w, in0=w, scalar1=per_row[:, TILES + n : TILES + n + 1], scalar2=None, op0=ALU.mult
-                )
-            store_if_whole(weighted, w_tiles, s, 1)
+                nc.vector.tensor_scalar(out=w, in0=w, scalar1=factor, scalar2=None, op0=ALU.mult)
+            store(weighted, w_tiles, s)
 
         issued = AHEAD
         for s in range(len(steps) + LAG_P):
@@ -350,9 +289,13 @@ def tile_cluster_expansion_reweighting_s2_kernel(
             for laid in pending:
                 quantize(laid)
             while issued < len(steps) and MUL_AT.get(issued, issued - LEAD) <= s:
-                multiply_step(issued)
+                multiply(issued, range(PASSES))
                 issued = issued + 1
             for stage_fn, lag in [(exponentiate, LAG_X), (add_field, 0), (times_prop, LAG_P)]:
                 if 0 <= s - lag < len(steps):
                     stage_fn(s - lag)
-            pending = [lay_out(item) for item in prepare.get(s, [])]
+            pending = []
+            if s in ECI_AT:
+                pending = [turn_eci(g, ECI_AT[s]) for g in (1, 2, 3)]
+            if s in corr_at:
+                pending.append(interleave_corr(*corr_at[s]))

from contextlib import ExitStack

import concourse.mybir as mybir
from concourse.masks import make_identity

M, N, KP, KB = 2048, 1024, 512, 1536
FLOPS = 2 * M * N * (KP + KB)

F32 = mybir.dt.float32
BF16 = mybir.dt.bfloat16
U32 = mybir.dt.uint32
U8 = mybir.dt.uint8
E4M3 = mybir.dt.float8_e4m3fn_x4
E5M2 = mybir.dt.float8_e5m2_x4
ACT = mybir.ActivationFunctionType
ALU = mybir.AluOpType

P = 128
PACK = 4
K_PASS = P * PACK
PASSES = (KP + KB) // K_PASS
BANK = 512
HALVES = N // BANK
BLOCK = 256
TILES = M // P
LOADS = [(0, 512), (512, 512), (1024, 1024)]
SLOTS = 15
LAG_T = 1
LAG_X = 2
LAG_P = 3
WLAG = (1, 1, 2)
AHEAD = 2
LEAD = 1
SUM_BANKS = 4
CORR_AT = [2, 4, 6, 8, 9, 10, 11, 12, 13, 14, 15, 16]
P_ON_S = [4, 5, 6, 7, 8, 10, 12, 14]
ECI_AT = {1: 2, 3: 3}
MUL_AT = {2: 2, 3: 2, 4: 4}
HEAD_S = (True, True)
E_ON_V = []


def tile_cluster_expansion_reweighting_s2_kernel(
    tc, pair_corr, body_corr, pair_eci, body_eci, field, prop, beta, energy, weighted
):
    nc = tc.nc

    with ExitStack() as ctx:
        keep = ctx.enter_context(tc.tile_pool(name="keep", bufs=1))
        ring = ctx.enter_context(tc.tile_pool(name="ring", bufs=SLOTS))
        stage = ctx.enter_context(tc.tile_pool(name="stage", bufs=4))
        turn_banks = ctx.enter_context(tc.psum_pool(name="turn_banks", bufs=8 - SUM_BANKS))
        sum_banks = ctx.enter_context(tc.psum_pool(name="sum_banks", bufs=SUM_BANKS))
        ctx.enter_context(tc.manual_schedule())

        ident = keep.tile([P, P], F32)
        make_identity(nc, ident[:])
        ident_bf16 = keep.tile([P, P], BF16)
        make_identity(nc, ident_bf16[:])
        vec_rows = keep.tile([P, P], BF16)
        nc.gpsimd.memset(vec_rows[:], 0.0)
        warm = keep.tile([P, 2], F32)
        nc.vector.memset(warm[:], 0.0)
        nc.scalar.activation(out=warm[:, 1:2], in_=warm[:, 0:1], func=ACT.Exp)

        raw_corr = {}
        raw_two = {}
        raw_pair = {}
        raw_body = {}
        beta_rows = keep.tile([P, N // P], BF16)

        def load_corr(g, first, width):
            rows = pair_corr if g == 0 else body_corr[(g - 1) * K_PASS : g * K_PASS, :]
            if g % 2 == 0:
                raw_two[first] = keep.tile([P, 2, PACK, width], BF16, name="raw_corr%d_%d" % (g, first))
            raw = raw_two[first]
            nc.sync.dma_start(
                out=raw[:, g % 2], in_=rows.rearrange("(p t) c -> p t c", t=PACK)[:, :, first : first + width]
            )
            for c in range(0, width, BLOCK):
                raw_corr[g // 2, (first + c) // BLOCK] = raw[:, :, :, c : c + BLOCK]

        def load_pair(h):
            raw = ring.tile([P, 2, 2 * KP], BF16, name="raw_pair", tag="slot")
            rows = pair_eci[h * BANK : (h + 1) * BANK, :]
            nc.sync.dma_start(out=raw[:], in_=rows.rearrange("(b p r) k -> p b (r k)", b=2, r=2))
            raw_pair[h] = raw

        def load_body(b):
            raw = keep.tile([P, 2 * KB], BF16, name="raw_body%d" % b)
            rows = body_eci[b * BLOCK : (b + 1) * BLOCK, :]
            nc.sync.dma_start(out=raw[:], in_=rows.rearrange("(p r) k -> p (r k)", r=2))
            raw_body[b] = raw

        load_corr(0, *LOADS[0])
        load_pair(0)
        load_body(0)
        load_body(1)
        load_corr(1, *LOADS[0])
        nc.sync.dma_start(out=beta_rows[:], in_=beta.rearrange("(p w) -> p w", p=P))
        nc.sync.dma_start(out=vec_rows[0:TILES, :], in_=field.rearrange("(n p) -> n p", p=P))
        nc.sync.dma_start(out=vec_rows[TILES : 2 * TILES, :], in_=prop.rearrange("(n p) -> n p", p=P))
        load_corr(2, *LOADS[0])
        load_corr(3, *LOADS[0])
        load_pair(1)
        load_body(2)
        load_body(3)
        for first, width in LOADS[1:]:
            for g in range(PASSES):
                load_corr(g, first, width)

        eci_codes = {}
        eci_scales = {}
        corr_codes = {}
        corr_scales = {}
        for g in range(PASSES):
            for h in range(HALVES):
                eci_codes[g, h] = keep.tile([P, BANK], U32, name="ec%d_%d" % (g, h), align_bytes=64)
                eci_scales[g, h] = keep.tile([P, BANK], U8, name="es%d_%d" % (g, h), align_bytes=64)
        for two in range(PASSES // 2):
            for b in range(M // BLOCK):
                corr_codes[two, b] = keep.tile([P, 2 * BLOCK], U32, name="cc%d_%d" % (two, b), align_bytes=64)
                corr_scales[two, b] = keep.tile([P, 2 * BLOCK], U8, name="cs%d_%d" % (two, b), align_bytes=64)

        def turn_eci(g, b):
            if g == 0:
                words = raw_pair[b // 2][:, b % 2, :].bitcast(F32)
                first, row = 0, KP // 2
            else:
                words = raw_body[b][:].bitcast(F32)
                first, row = (g - 1) * (K_PASS // 2), KB // 2
            bank = turn_banks.tile([P, BANK], F32, name="turned")
            for r in range(2):
                for u in range(2):
                    start = r * row + first
                    j = 2 * r + u
                    nc.tensor.transpose(
                        bank[:, j * P : (j + 1) * P], words[:, start + u : start + K_PASS // 2 : 2], ident[:]
                    )
            grouped = stage.tile([P, BLOCK * PACK], BF16, name="eci_grouped", align_bytes=64)
            nc.scalar.copy(
                out=grouped[:].bitcast(F32).rearrange("p (n j) -> p n j", j=4),
                in_=bank[:].rearrange("p (j n) -> p n j", j=4),
            )
            cols = slice((b % 2) * BLOCK, (b % 2 + 1) * BLOCK)
            return eci_codes[g, b // 2][:, cols].bitcast(E4M3 if g == 0 else E5M2), eci_scales[g, b // 2][:, cols], grouped

        def interleave_corr(passes, b, on_scalar=False):
            two, first = divmod(passes[0], 2)
            count = len(passes)
            grouped = stage.tile([P, count * BLOCK * PACK], BF16, name="corr_grouped", bufs=4, align_bytes=64)
            dst = grouped[:].rearrange("p (g c i t) -> p g c t i", g=count, i=4, t=PACK)
            src = raw_corr[two, b][:, first : first + count].rearrange("p g t (c i) -> p g c t i", i=4)
            if on_scalar:
                nc.scalar.copy(out=dst, in_=src)
            else:
                nc.vector.tensor_copy(out=dst, in_=src)
            cols = slice(first * BLOCK, (first + count) * BLOCK)
            return corr_codes[two, b][:, cols].bitcast(E4M3), corr_scales[two, b][:, cols], grouped

        def quantize(laid):
            codes, scales, grouped = laid
            nc.vector.quantize_mx(out=codes, scales=scales, in_=grouped[:])

        first_tiles = LOADS[0][1] // P
        steps = [(n, (h,)) for h in range(HALVES) for n in range(first_tiles)]
        steps = steps + [(n, (0, 1)) for n in range(first_tiles, TILES - 1)]
        steps = steps + [(TILES - 1, (h,)) for h in range(HALVES)]
        sums = {}

        def multiply(s, passes):
            n, halves = steps[s]
            b, i = divmod(n, BLOCK // P)
            for h in halves:
                for g in passes:
                    if g == 0:
                        sums[n, h] = sum_banks.tile([P, BANK], F32, name="sums")
                    first = (g % 2) * BLOCK + i * P
                    cols = slice(first, first + P)
                    nc.tensor.matmul_mx(
                        out=sums[n, h][:],
                        lhsT=corr_codes[g // 2, b][:, cols].bitcast(E4M3),
                        lhsT_scale=corr_scales[g // 2, b][:, cols],
                        rhs=eci_codes[g, h][:].bitcast(E4M3 if g == 0 else E5M2),
                        rhs_scale=eci_scales[g, h][:],
                        start=(g == 0),
                        stop=(g == PASSES - 1),
                    )

        beta_all = keep.tile([P, N], BF16)
        per_row = keep.tile([P, 2 * TILES], F32)

        def spread_vectors():
            bank = turn_banks.tile([P, BANK], F32, name="turned")
            beta_words = beta_rows[:].bitcast(F32)
            for w in range(4):
                nc.tensor.transpose(
                    bank[:, w * P : (w + 1) * P], beta_words[:, w : w + 1].to_broadcast([P, P]), ident[:]
                )
            nc.scalar.copy(
                out=beta_all[:].bitcast(F32).rearrange("p (n w) -> p n w", w=4),
                in_=bank[:].rearrange("p (w n) -> p n w", w=4),
            )
            bank = turn_banks.tile([P, BANK], F32, name="turned")
            columns = bank[:, 0 : P // 2].bitcast(BF16)
            nc.tensor.transpose(columns, vec_rows[:], ident_bf16[:])
            nc.scalar.copy(out=per_row[:], in_=columns[:, 0 : 2 * TILES])

        c0 = [interleave_corr((0,), b) for b in (0, 1)]
        pair = [turn_eci(0, b) for b in (0, 1)]
        for laid in c0 + pair:
            quantize(laid)
        for laid in [turn_eci(g, 0) for g in (1, 2, 3)]:
            quantize(laid)
        body = [turn_eci(g, 1) for g in (1, 2, 3)]
        c1 = [interleave_corr((1,), b) for b in (0, 1)]
        spread_vectors()
        for laid in [body[0], c1[0], body[1], c1[1], body[2]]:
            quantize(laid)
        for s in range(AHEAD):
            multiply(s, (0, 1))
        c2 = interleave_corr((2,), 0)
        c2_late = interleave_corr((2,), 1, HEAD_S[0])
        c3 = interleave_corr((3,), 0)
        quantize(c2)
        c3_late = interleave_corr((3,), 1, HEAD_S[1])
        pair = [turn_eci(0, b) for b in (2, 3)]
        quantize(c3)
        for s in range(AHEAD):
            multiply(s, (2, 3))
        pending = [c2_late, c3_late] + pair

        later = [(passes, b) for b in range(LOADS[0][1] // BLOCK, M // BLOCK) for passes in ((0, 1), (2, 3))]
        corr_at = dict(zip(CORR_AT, later))

        e_tiles = {}
        w_tiles = {}

        def draws(s):
            halves = steps[s][1]
            return slice(halves[0] * BANK, (halves[-1] + 1) * BANK)

        def piece(tiles, s):
            return tiles[steps[s][0]][:, draws(s)]

        def store(out, tiles, s):
            n, halves = steps[s]
            if n == TILES - 1:
                nc.sync.dma_start(out=out[n * P : (n + 1) * P, draws(s)], in_=piece(tiles, s))
            elif halves[-1] == HALVES - 1:
                nc.sync.dma_start(out=out[n * P : (n + 1) * P, :], in_=tiles[n][:])

        def add_field(s):
            n, halves = steps[s]
            if halves[0] == 0:
                e_tiles[n] = ring.tile([P, N], F32, name="e_tile", tag="slot")
                w_tiles[n] = ring.tile([P, N], F32, name="w_tile", tag="slot")
            for h in halves:
                e = e_tiles[n][:, h * BANK : (h + 1) * BANK]
                if (n, h) in E_ON_V:
                    nc.vector.tensor_scalar(
                        out=e, in0=sums[n, h][:], scalar1=per_row[:, n : n + 1], scalar2=None, op0=ALU.add
                    )
                else:
                    nc.scalar.activation(out=e, in_=sums[n, h][:], func=ACT.Identity, bias=per_row[:, n : n + 1])
            store(energy, e_tiles, s)

        def times_beta(s):
            nc.vector.tensor_tensor(out=piece(w_tiles, s), in0=piece(e_tiles, s), in1=beta_all[:, draws(s)], op=ALU.mult)

        def exponentiate(s):
            w = piece(w_tiles, s)
            nc.scalar.activation(out=w, in_=w, func=ACT.Exp, scale=-1.0)

        def times_prop(s):
            n = steps[s][0]
            w = piece(w_tiles, s)
            factor = per_row[:, TILES + n : TILES + n + 1]
            if s in P_ON_S:
                nc.scalar.activation(out=w, in_=w, func=ACT.Identity, scale=factor)
            else:
                nc.vector.tensor_scalar(out=w, in0=w, scalar1=factor, scalar2=None, op0=ALU.mult)
            store(weighted, w_tiles, s)

        issued = AHEAD
        for s in range(len(steps) + LAG_P):
            if 0 <= s - LAG_T < len(steps):
                times_beta(s - LAG_T)
            for laid in pending:
                quantize(laid)
            while issued < len(steps) and MUL_AT.get(issued, issued - LEAD) <= s:
                multiply(issued, range(PASSES))
                issued = issued + 1
            for stage_fn, lag in [(exponentiate, LAG_X), (add_field, 0), (times_prop, LAG_P)]:
                if 0 <= s - lag < len(steps):
                    stage_fn(s - lag)
            pending = []
            if s in ECI_AT:
                pending = [turn_eci(g, ECI_AT[s]) for g in (1, 2, 3)]
            if s in corr_at:
                pending.append(interleave_corr(*corr_at[s]))
